import numpy as np
import ml_dtypes


def mxq(x, axis, fmt="e4m3"):
    dtype, down = {"e4m3": (ml_dtypes.float8_e4m3fn, 7), "e5m2": (ml_dtypes.float8_e5m2, 14)}[fmt]
    v = np.moveaxis(np.asarray(x, np.float32).astype(ml_dtypes.bfloat16).astype(np.float64), axis, -1)
    blocks = v.reshape(v.shape[:-1] + (-1, 32))
    amax = np.abs(blocks).max(-1, keepdims=True)
    byte = np.maximum(np.where(amax > 0, np.frexp(amax)[1] - 1 + 127, 0) - down, 1)
    scale = np.exp2(byte - 127.0)
    codes = (blocks / scale).astype(np.float32).astype(dtype).astype(np.float64)
    return np.moveaxis((codes * scale).reshape(v.shape), -1, axis)


WIDE = False


def mx_kscale(k):
    if not WIDE:
        return np.ones(k)
    levels = np.array([10, -10, 5, -5, 0])
    if k % 512:
        return np.exp2(np.random.permutation(np.resize(levels, k // 32))).repeat(32)
    a = np.empty((k // 512, 16))
    for p in range(k // 512):
        a[p, :8] = np.random.permutation(np.resize(levels, 8))
        for g in range(8):
            far = levels[np.abs(levels - a[p, g]) >= 10]
            a[p, g + 8] = far[np.random.randint(len(far))]
    return np.exp2(a.ravel()).repeat(32)


def f64(x):
    return np.asarray(x).astype(np.float64)


def striped(idx):
    return np.tile(idx.reshape(-1, 16).T, (8, 1)).astype(np.uint16)


def unstriped(offs):
    return offs[:16].T.reshape(-1).astype(np.int64)


def striped8(idx):
    return np.concatenate([x.reshape(-1, 16).T for x in idx]).astype(np.uint16)


def runs(offs, k):
    lists = np.stack([offs[16 * r : 16 * r + 16].T.reshape(-1) for r in range(8)]).astype(np.int64)
    return lists[np.arange(k) % 512 // 64]


def pack_weight(w):
    k, n = w.shape
    w = f64(np.asarray(w, np.float32).astype(ml_dtypes.bfloat16)).reshape(k // 32, 32, n)
    amax = np.abs(w).max(1)
    byte = np.clip(np.where(amax > 0, np.frexp(amax)[1] - 1 + 127 - 7, 1), 1, 254)
    scaled = (w * np.exp2(127.0 - byte)[:, None, :]).reshape(k, n).astype(np.float32)
    words = np.ascontiguousarray(scaled.reshape(k // 512, 128, 4, n).transpose(0, 1, 3, 2)).astype(ml_dtypes.float8_e4m3fn).view(np.uint8)
    return words, np.ascontiguousarray(byte.astype(np.uint8).reshape(k // 512, 16, n))


def unpack_weight(words, scales):
    g, p, n, _ = words.shape
    vals = np.ascontiguousarray(words).view(ml_dtypes.float8_e4m3fn).astype(np.float64) * np.repeat(np.exp2(scales.astype(np.float64) - 127.0), 8, axis=1)[..., None]
    return vals.transpose(0, 1, 3, 2).reshape(g * 512, n)


E2M1 = np.array([0.0, 0.5, 1.0, 1.5, 2.0, 3.0, 4.0, 6.0, -0.0, -0.5, -1.0, -1.5, -2.0, -3.0, -4.0, -6.0])


def pack_fp4(w):
    k, n = w.shape
    w = f64(np.asarray(w, np.float32).astype(ml_dtypes.bfloat16)).reshape(k // 32, 32, n)
    amax = np.abs(w).max(1)
    mant, ex = np.frexp(amax / 6.0)
    byte = np.clip(np.where(amax > 0, np.where(mant > 0.5, ex, ex - 1) + 127, 1), 1, 254)
    scaled = (w * np.exp2(127.0 - byte)[:, None, :]).reshape(k, n).astype(np.float32)
    c = np.ascontiguousarray(scaled.reshape(k // 512, 128, 4, n).transpose(0, 1, 3, 2)).astype(ml_dtypes.float4_e2m1fn).view(np.uint8) & 0xF
    words = (c[..., 0::2] | (c[..., 1::2] << 4)).reshape(k // 512, 128, 2 * n)
    return np.ascontiguousarray(words), np.ascontiguousarray(byte.astype(np.uint8).reshape(k // 512, 16, n))


def unpack_fp4(words, scales):
    g, _, n = scales.shape
    words = np.ascontiguousarray(words).reshape(g, 128, n, 2)
    nib = np.empty((g, 128, n, 4), np.uint8)
    nib[..., 0::2] = words & 0xF
    nib[..., 1::2] = words >> 4
    vals = E2M1[nib] * np.repeat(np.exp2(scales.astype(np.float64) - 127.0), 8, axis=1)[..., None]
    return vals.transpose(0, 1, 3, 2).reshape(g * 512, n)


def planes(y):
    n, m = y.shape
    v = y.astype(np.float32).astype(ml_dtypes.bfloat16).astype(np.float64).reshape(n // 32, 32, m)
    top = np.abs(v).max(1)
    byte = np.clip(np.where(top > 0, np.frexp(top)[1] - 1 + 127 - 7, 1), 1, 254)
    codes = (v * np.exp2(127.0 - byte)[:, None, :]).reshape(n, m).astype(np.float32).astype(ml_dtypes.float8_e4m3fn).view(np.uint8)
    words = codes.reshape(n // 512, 128, 4, m).transpose(0, 1, 3, 2)
    return np.ascontiguousarray(words), np.ascontiguousarray(byte.astype(np.uint8).reshape(n // 512, 16, m))


K, T, S, N, H, U = 512, 2048, 512, 512, 512, 1024


def setup_inputs():
    n = np.random.standard_normal
    s = mx_kscale(K)[:, None]
    u = mx_kscale(H)
    packed_xT = pack_weight(n((K, T)) * s)
    packed_w1 = pack_fp4(n((K, H)) / np.sqrt(K) / s)
    packed_w2 = pack_fp4(n((K, H)) / np.sqrt(K) / s)
    packed_w3 = pack_fp4(n((H, N)) / np.sqrt(H) / u[:, None])
    return {
        "x_words": packed_xT[0],
        "x_scales": packed_xT[1],
        "w1_words": packed_w1[0],
        "w1_scales": packed_w1[1],
        "w2_words": packed_w2[0],
        "w2_scales": packed_w2[1],
        "gn": (np.random.uniform(0.5, 1.5, (H, 1)) * u[:, None]).astype(np.float32),
        "w3_words": packed_w3[0],
        "w3_scales": packed_w3[1],
        "mem": n((N, U)).astype(np.float32),
        "offs": striped(np.random.permutation(T)[:S]),
        "two": striped(np.random.permutation(T)[:S]),
        "n1": striped8(np.stack([np.random.permutation(S) for _ in range(8)])),
        "n2": striped8(np.stack([np.random.permutation(S) for _ in range(8)])),
        "n3": striped8(np.stack([np.random.permutation(U)[:S] for _ in range(8)])),
    }


def reference(x_words, x_scales, w1_words, w1_scales, w2_words, w2_scales, gn, w3_words, w3_scales, mem, offs, two, n1, n2, n3):
    xq = unpack_weight(x_words, x_scales)[:, unstriped(offs)]
    y = unpack_fp4(w1_words, w1_scales).T @ xq
    x_two = unpack_weight(x_words, x_scales)[:, unstriped(two)]
    d = unpack_fp4(w2_words, w2_scales).T @ x_two
    z = f64(gn) * (np.maximum(y, d[np.arange(H)[:, None], runs(n2, H)]) - (np.minimum(y[np.arange(H)[:, None], runs(n1, H)], d)))
    h = unpack_fp4(w3_words, w3_scales).T @ mxq(z, 0, "e4m3")
    out = f64(mem).copy()
    out[np.arange(N)[:, None], runs(n3, N)] = h
    return (out,) + planes(out)

@@ -1,0 +1,210 @@
+from contextlib import ExitStack
+
+import concourse.mybir as mybir
+from concourse.masks import make_identity
+
+F32 = mybir.dt.float32
+BF16 = mybir.dt.bfloat16
+I32 = mybir.dt.int32
+U32 = mybir.dt.uint32
+U16 = mybir.dt.uint16
+U8 = mybir.dt.uint8
+FP8X4 = mybir.dt.float8_e4m3fn_x4
+FP4X4 = mybir.dt.float4_e2m1fn_x4
+ALU = mybir.AluOpType
+ACT = mybir.ActivationFunctionType
+
+P = 128
+PACK = 4
+T, S, U = 2048, 512, 1024
+HALF = S // 2
+FLOPS = 3 * 2 * 512 * 512 * 512
+
+
+def tile_picked_twlmaxbpage_none_po_kernel(tc, x_words, x_scales, w1_words, w1_scales, w2_words, w2_scales, gn, w3_words, w3_scales, mem, offs, two, n1, n2, n3, out_0, out_1, out_2):
+    nc = tc.nc
+    with ExitStack() as ctx:
+        keep = ctx.enter_context(tc.tile_pool(name="keep", bufs=1))
+        work = ctx.enter_context(tc.tile_pool(name="work", bufs=2))
+        psum = ctx.enter_context(tc.psum_pool(name="psum", bufs=3))
+        banks = ctx.enter_context(tc.psum_pool(name="banks", bufs=1))
+
+        def load_list(src, name):
+            t = keep.tile([P, S // 16], U16, name=name)
+            nc.sync.dma_start(t[:], src)
+            return t
+
+        def load_scale_rows(dst, src, queue):
+            for q in range(4):
+                queue.dma_start(dst[32 * q : 32 * q + 4, :].bitcast(I32), src[0, 4 * q : 4 * q + 4, :].bitcast(I32))
+
+        xs = keep.tile([P, T], U8, name="xs", tag="slot2", align_bytes=64)
+        nc.vector.memset(xs[:].bitcast(I32), 0)
+        ws_raw = [keep.tile([P, S], U8, name="ws_raw%d" % i, tag=("slot0", "slot1", "ws_raw2")[i], align_bytes=64) for i in range(3)]
+        for i in range(3):
+            nc.vector.memset(ws_raw[i][:].bitcast(I32), 0)
+
+        xw = keep.tile([P, T], I32, name="xw", align_bytes=64)
+        ww_raw = [keep.tile([P, 2 * S], U8, name="ww_raw%d" % i, tag=("ww_raw0", "slot3")[i], align_bytes=64) for i in range(2)]
+        offs_t = load_list(offs, "offs_t")
+        two_t = load_list(two, "two_t")
+        nc.sync.dma_start(ww_raw[0][:].bitcast(I32), w1_words[0].bitcast(I32))
+        load_scale_rows(xs, x_scales, nc.sync)
+        nc.sync.dma_start(xw[:], x_words[0].rearrange("p n t -> p (n t)").bitcast(I32))
+        gn_t = keep.tile([P, PACK], F32, name="gn_t")
+        nc.gpsimd.dma_start(gn_t[:], gn.rearrange("(p t) o -> p (t o)", t=PACK))
+        load_scale_rows(ws_raw[0], w1_scales, nc.sync)
+        nc.sync.dma_start(ww_raw[1][:].bitcast(I32), w2_words[0].bitcast(I32))
+        load_scale_rows(ws_raw[1], w2_scales, nc.sync)
+        n1_t = load_list(n1, "n1_t")
+        n2_t = load_list(n2, "n2_t")
+
+        ww = [keep.tile([P, 2 * S], U8, name="ww%d" % i, align_bytes=64) for i in range(3)]
+        ws = [keep.tile([P, S], U8, name="ws%d" % i, align_bytes=64) for i in range(3)]
+
+        def deal(i, engine):
+            engine.tensor_copy(ww[i][:].rearrange("p (t m b) -> p t m b", t=PACK, b=2), ww_raw[i][:].rearrange("p (m t b) -> p t m b", t=PACK, b=2))
+            engine.tensor_copy(ws[i][:].rearrange("p (t m) -> p t m", t=PACK), ws_raw[i][:].rearrange("p (m t) -> p t m", t=PACK))
+
+        deal(0, nc.gpsimd)
+        deal(1, nc.gpsimd)
+        ww_raw.append(keep.tile([P, 2 * S], U8, name="ww_raw2", tag="ww_raw0", align_bytes=64))
+        nc.sync.dma_start(ww_raw[2][:].bitcast(I32), w3_words[0].bitcast(I32))
+        load_scale_rows(ws_raw[2], w3_scales, nc.sync)
+        n3_t = load_list(n3, "n3_t")
+
+        lists = [offs_t, two_t]
+        xg = [keep.tile([P, S], U32, name="xg%d" % i, align_bytes=64) for i in range(2)]
+        sg = [keep.tile([P, S], U8, name="sg%d" % i, align_bytes=64) for i in range(2)]
+        for i in range(2):
+            nc.vector.tensor_copy(sg[i][:], xs[:].indirect(lists[i][:]))
+        for i in range(2):
+            nc.vector.tensor_copy(xg[i][:], xw[:].bitcast(U32).indirect(lists[i][:]))
+        deal(2, nc.vector)
+
+        mem_rows = mem.rearrange("(p t) w -> p t w", t=PACK)
+        out_rows = out_0.rearrange("(p t) w -> p t w", t=PACK)
+        page = [keep.tile([P, U], F32, name="page%d" % t, tag="slot%d" % t, align_bytes=64) for t in range(PACK)]
+        for t in range(PACK):
+            nc.sync.dma_start(page[t][:], mem_rows[:, t, :])
+
+        def product(i, t, acc, codes, scales):
+            nc.tensor.matmul_mx(out=acc, lhsT=ww[i][:, 2 * P * t : 2 * P * (t + 1)].bitcast(FP4X4), lhsT_scale=ws[i][:, P * t : P * (t + 1)], rhs=codes.bitcast(FP8X4), rhs_scale=scales, start=True, stop=True)
+
+        ident = keep.tile([P, P], F32, name="ident")
+        make_identity(nc, ident[:])
+        mag = keep.tile([P, PACK], F32, name="mag")
+        neg = keep.tile([P, PACK], F32, name="neg")
+        sgn = keep.tile([P, PACK], BF16, name="sgn")
+        nc.scalar.activation(mag[:], gn_t[:], ACT.Abs)
+        nc.scalar.activation(neg[:], mag[:], ACT.Copy, scale=-1.0)
+        nc.scalar.activation(sgn[:], gn_t[:], ACT.Sign)
+
+        y = [keep.tile([P, S], F32, name="y%d" % t) for t in range(PACK)]
+        nd = [keep.tile([P, S], F32, name="nd%d" % t) for t in range(PACK)]
+        for t in range(PACK):
+            for i, dst, scale in ((0, y, mag), (1, nd, neg)):
+                acc = psum.tile([P, S], F32, name="acc")
+                product(i, t, acc[:], xg[i][:], sg[i][:])
+                nc.scalar.activation(dst[t][:], acc[:], ACT.Copy, scale=scale[:, t : t + 1])
+
+        sums = [banks.tile([P, PACK, P], F32, name="sum%d" % b) for b in range(4)]
+
+        def add_turned(b, t, src, start, stop):
+            nc.tensor.matmul(sums[b][:, t, :], lhsT=src, rhs=ident[:], is_transpose=True, start=start, stop=stop)
+
+        def plain_terms(hf):
+            for t in range(PACK):
+                for b in (2 * hf, 2 * hf + 1):
+                    add_turned(b, t, nd[t][:, b * P : (b + 1) * P], t == 0, False)
+                    add_turned(b, t, y[t][:, b * P : (b + 1) * P], False, False)
+
+        zi = [work.tile([P, HALF, PACK], BF16, name="zi%d" % hf, tag="zi%d" % hf, bufs=1, align_bytes=64) for hf in range(2)]
+
+        def looked_up_terms(hf, t):
+            cols = slice(hf * HALF, (hf + 1) * HALF)
+            lc = slice(hf * HALF // 16, (hf + 1) * HALF // 16)
+            if (hf, t) == (1, PACK - 1):
+                pre = work.tile([P, 2, HALF], F32, name="pre_last", tag="zi0", bufs=1, align_bytes=64)
+            else:
+                pre = work.tile([P, 2, HALF], F32, name="pre", bufs=4)
+            nc.vector.tensor_tensor(pre[:, 0, :], y[t][:].indirect(n1_t[:, lc]), nd[t][:, cols], ALU.add)
+            nc.vector.tensor_tensor(pre[:, 1, :], nd[t][:].indirect(n2_t[:, lc]), y[t][:, cols], ALU.add)
+            cut = work.tile([P, 2, HALF], F32, name="cut", bufs=4)
+            nc.scalar.activation(cut[:], pre[:], ACT.Relu, scale=-1.0)
+            for c in range(2):
+                for i in range(2):
+                    add_turned(2 * hf + c, t, cut[:, i, c * P : (c + 1) * P], False, t == PACK - 1 and i == 1)
+
+        zq = [keep.tile([P, HALF], U32, name="zq%d" % hf, align_bytes=64) for hf in range(2)]
+        zs = [keep.tile([P, HALF], U8, name="zs%d" % hf, align_bytes=64) for hf in range(2)]
+
+        def quantise(hf):
+            back = banks.tile([P, 2, HALF], F32, name="back")
+            for c in range(2):
+                zt = work.tile([P, S], BF16, name="zt", bufs=2)
+                nc.scalar.copy(zt[:].rearrange("j (u p e) -> j u p e", u=2, e=2), sums[2 * hf + c][:].rearrange("j (u e) p -> j u p e", u=2))
+                for u in range(2):
+                    nc.tensor.transpose(back[:, u, c * P : (c + 1) * P], zt[:].bitcast(F32)[:, u * P : (u + 1) * P], ident[:])
+            nc.vector.tensor_tensor(
+                zi[hf][:].rearrange("p j (u e) -> p j u e", u=2),
+                back[:].rearrange("p u j -> p (u j)").bitcast(BF16).rearrange("p (u j e) -> p j u e", u=2, e=2),
+                sgn[:].rearrange("p (u e) -> p u e", u=2).unsqueeze(1).to_broadcast([P, HALF, 2, 2]),
+                ALU.mult,
+            )
+            nc.vector.quantize_mx(out=zq[hf][:].bitcast(FP8X4), scales=zs[hf][:], in_=zi[hf][:].rearrange("p j t -> p (j t)"))
+
+        h = [[None] * PACK, [None] * PACK]
+
+        def second_product(hf, u):
+            if (hf, u) == (0, 1):
+                acc = banks.tile([P, 2, HALF], F32, name="acc_late", tag="sum3")
+            else:
+                acc = psum.tile([P, 2, HALF], F32, name="acc")
+            for e in range(2):
+                product(2, 2 * u + e, acc[:, e, :], zq[hf][:], zs[hf][:])
+            hs = keep.tile([P, 2, HALF], F32, name="hs%d_%d" % (hf, u))
+            nc.scalar.copy(hs[:], acc[:])
+            h[hf][2 * u] = hs[:, 0, :]
+            h[hf][2 * u + 1] = hs[:, 1, :]
+
+        plain_terms(0)
+        for t in range(PACK):
+            looked_up_terms(0, t)
+        plain_terms(1)
+        quantise(0)
+        second_product(0, 0)
+        for t in range(PACK):
+            looked_up_terms(1, t)
+        quantise(1)
+        second_product(0, 1)
+        second_product(1, 0)
+        second_product(1, 1)
+
+        SPLIT = U // 2
+        grouped = keep.tile([P, U, PACK], BF16, name="grouped", align_bytes=64)
+        staged = keep.tile([P, PACK, SPLIT], BF16, name="staged", align_bytes=64)
+        last = PACK - 1
+        for hf, t in ((0, 0), (0, 1), (0, 2), (1, 0), (1, 1), (1, 2), (0, 3), (1, 3)):
+            lc = slice(hf * HALF // 16, (hf + 1) * HALF // 16)
+            nc.vector.tensor_copy(page[t][:].indirect(n3_t[:, lc]), h[hf][t])
+            if hf == 1:
+                nc.sync.dma_start(out_rows[:, t, :], page[t][:])
+                if t < last:
+                    nc.scalar.copy(staged[:, t, :], page[t][:, :SPLIT])
+                    nc.scalar.copy(grouped[:, SPLIT:, t], page[t][:, SPLIT:])
+        oq = keep.tile([P, U], U32, name="oq", align_bytes=64)
+        osc = keep.tile([P, U], U8, name="osc", align_bytes=64)
+        words_out = out_1[0].rearrange("p n t -> p (n t)").bitcast(I32)
+        Q = U // 4
+        nc.vector.tensor_copy(staged[:, last, :], page[last][:, :SPLIT])
+        for c in (2, 3):
+            nc.scalar.copy(grouped[:, c * Q : (c + 1) * Q, last], page[last][:, c * Q : (c + 1) * Q])
+        for c in (0, 1):
+            nc.vector.tensor_copy(grouped[:, c * Q : (c + 1) * Q, :].rearrange("p (c i) t -> p c t i", i=4), staged[:, :, c * Q : (c + 1) * Q].rearrange("p t (c i) -> p c t i", i=4))
+        for c in (2, 0, 3, 1):
+            cs = slice(c * Q, (c + 1) * Q)
+            nc.vector.quantize_mx(out=oq[:, cs].bitcast(FP8X4), scales=osc[:, cs], in_=grouped[:, cs, :].rearrange("p j t -> p (j t)"))
+            nc.sync.dma_start(words_out[:, cs], oq[:, cs].bitcast(I32))
+        for q in range(4):
+            nc.scalar.dma_start(out_2[0, 4 * q : 4 * q + 4, :].bitcast(I32), osc[32 * q : 32 * q + 4, :].bitcast(I32))

@@ -25,8 +25,6 @@ def tile_picked_twlmaxbpage_none_po_kernel(tc, x_words, x_scales, w1_words, w1_s
     nc = tc.nc
     with ExitStack() as ctx:
         keep = ctx.enter_context(tc.tile_pool(name="keep", bufs=1))
-        work = ctx.enter_context(tc.tile_pool(name="work", bufs=2))
-        psum = ctx.enter_context(tc.psum_pool(name="psum", bufs=3))
         banks = ctx.enter_context(tc.psum_pool(name="banks", bufs=1))
 
         def load_list(src, name):
@@ -34,59 +32,56 @@ def tile_picked_twlmaxbpage_none_po_kernel(tc, x_words, x_scales, w1_words, w1_s
             nc.sync.dma_start(t[:], src)
             return t
 
-        def load_scale_rows(dst, src, queue):
+        def load_scale_rows(dst, src):
             for q in range(4):
-                queue.dma_start(dst[32 * q : 32 * q + 4, :].bitcast(I32), src[0, 4 * q : 4 * q + 4, :].bitcast(I32))
+                nc.sync.dma_start(dst[32 * q : 32 * q + 4, :].bitcast(I32), src[0, 4 * q : 4 * q + 4, :].bitcast(I32))
 
-        xs = keep.tile([P, T], U8, name="xs", tag="slot2", align_bytes=64)
+        xs = keep.tile([P, T], U8, name="xs", align_bytes=64)
         nc.vector.memset(xs[:].bitcast(I32), 0)
-        ws_raw = [keep.tile([P, S], U8, name="ws_raw%d" % i, tag=("slot0", "slot1", "ws_raw2")[i], align_bytes=64) for i in range(3)]
+        ws_raw = [keep.tile([P, S], U8, name="ws_raw%d" % i, tag=("ws_raw0", "ws_raw1", "slot3")[i], align_bytes=64) for i in range(3)]
         for i in range(3):
             nc.vector.memset(ws_raw[i][:].bitcast(I32), 0)
 
-        xw = keep.tile([P, T], I32, name="xw", align_bytes=64)
-        ww_raw = [keep.tile([P, 2 * S], U8, name="ww_raw%d" % i, tag=("ww_raw0", "slot3")[i], align_bytes=64) for i in range(2)]
+        xw = keep.tile([P, T], I32, name="xw", tag="xw", align_bytes=64)
+        ww_raw = [keep.tile([P, 2 * S], U8, name="ww_raw%d" % i, tag=("slot2", "ww_raw1")[i], align_bytes=64) for i in range(2)]
         offs_t = load_list(offs, "offs_t")
         two_t = load_list(two, "two_t")
         nc.sync.dma_start(ww_raw[0][:].bitcast(I32), w1_words[0].bitcast(I32))
-        load_scale_rows(xs, x_scales, nc.sync)
+        load_scale_rows(xs, x_scales)
         nc.sync.dma_start(xw[:], x_words[0].rearrange("p n t -> p (n t)").bitcast(I32))
         gn_t = keep.tile([P, PACK], F32, name="gn_t")
         nc.gpsimd.dma_start(gn_t[:], gn.rearrange("(p t) o -> p (t o)", t=PACK))
-        load_scale_rows(ws_raw[0], w1_scales, nc.sync)
+        load_scale_rows(ws_raw[0], w1_scales)
         nc.sync.dma_start(ww_raw[1][:].bitcast(I32), w2_words[0].bitcast(I32))
-        load_scale_rows(ws_raw[1], w2_scales, nc.sync)
+        load_scale_rows(ws_raw[1], w2_scales)
         n1_t = load_list(n1, "n1_t")
         n2_t = load_list(n2, "n2_t")
 
-        ww = [keep.tile([P, 2 * S], U8, name="ww%d" % i, align_bytes=64) for i in range(3)]
-        ws = [keep.tile([P, S], U8, name="ws%d" % i, align_bytes=64) for i in range(3)]
+        ww, ws = [], []
 
         def deal(i, engine):
+            ww.append(keep.tile([P, 2 * S], U8, name="ww%d" % i, tag=("ww0", "ww1", "xw")[i], align_bytes=64))
+            ws.append(keep.tile([P, S], U8, name="ws%d" % i, tag=("ws0", "ws1", "sg0")[i], align_bytes=64))
             engine.tensor_copy(ww[i][:].rearrange("p (t m b) -> p t m b", t=PACK, b=2), ww_raw[i][:].rearrange("p (m t b) -> p t m b", t=PACK, b=2))
             engine.tensor_copy(ws[i][:].rearrange("p (t m) -> p t m", t=PACK), ws_raw[i][:].rearrange("p (m t) -> p t m", t=PACK))
 
         deal(0, nc.gpsimd)
         deal(1, nc.gpsimd)
-        ww_raw.append(keep.tile([P, 2 * S], U8, name="ww_raw2", tag="ww_raw0", align_bytes=64))
+        ww_raw.append(keep.tile([P, 2 * S], U8, name="ww_raw2", tag="slot2", align_bytes=64))
         nc.sync.dma_start(ww_raw[2][:].bitcast(I32), w3_words[0].bitcast(I32))
-        load_scale_rows(ws_raw[2], w3_scales, nc.sync)
+        load_scale_rows(ws_raw[2], w3_scales)
         n3_t = load_list(n3, "n3_t")
 
         lists = [offs_t, two_t]
-        xg = [keep.tile([P, S], U32, name="xg%d" % i, align_bytes=64) for i in range(2)]
-        sg = [keep.tile([P, S], U8, name="sg%d" % i, align_bytes=64) for i in range(2)]
+        xg = [keep.tile([P, S], U32, name="xg%d" % i, tag="slot%d" % i, align_bytes=64) for i in range(2)]
+        sg = [keep.tile([P, S], U8, name="sg%d" % i, tag="sg%d" % i, align_bytes=64) for i in range(2)]
         for i in range(2):
             nc.vector.tensor_copy(sg[i][:], xs[:].indirect(lists[i][:]))
         for i in range(2):
             nc.vector.tensor_copy(xg[i][:], xw[:].bitcast(U32).indirect(lists[i][:]))
-        deal(2, nc.vector)
 
         mem_rows = mem.rearrange("(p t) w -> p t w", t=PACK)
         out_rows = out_0.rearrange("(p t) w -> p t w", t=PACK)
-        page = [keep.tile([P, U], F32, name="page%d" % t, tag="slot%d" % t, align_bytes=64) for t in range(PACK)]
-        for t in range(PACK):
-            nc.sync.dma_start(page[t][:], mem_rows[:, t, :])
 
         def product(i, t, acc, codes, scales):
             nc.tensor.matmul_mx(out=acc, lhsT=ww[i][:, 2 * P * t : 2 * P * (t + 1)].bitcast(FP4X4), lhsT_scale=ws[i][:, P * t : P * (t + 1)], rhs=codes.bitcast(FP8X4), rhs_scale=scales, start=True, stop=True)
@@ -102,35 +97,36 @@ def tile_picked_twlmaxbpage_none_po_kernel(tc, x_words, x_scales, w1_words, w1_s
 
         y = [keep.tile([P, S], F32, name="y%d" % t) for t in range(PACK)]
         nd = [keep.tile([P, S], F32, name="nd%d" % t) for t in range(PACK)]
-        for t in range(PACK):
-            for i, dst, scale in ((0, y, mag), (1, nd, neg)):
-                acc = psum.tile([P, S], F32, name="acc")
-                product(i, t, acc[:], xg[i][:], sg[i][:])
-                nc.scalar.activation(dst[t][:], acc[:], ACT.Copy, scale=scale[:, t : t + 1])
+        for i, t, bank in ((0, 0, "a"), (0, 1, "b"), (1, 0, "c"), (1, 1, "a"), (0, 2, "c"), (1, 2, "b"), (0, 3, "a"), (1, 3, "c")):
+            acc = banks.tile([P, S], F32, name="acc", tag=bank)
+            product(i, t, acc[:], xg[i][:], sg[i][:])
+            nc.scalar.activation((y, nd)[i][t][:], acc[:], ACT.Copy, scale=(mag, neg)[i][:, t : t + 1])
 
-        sums = [banks.tile([P, PACK, P], F32, name="sum%d" % b) for b in range(4)]
+        deal(2, nc.vector)
+        page = [keep.tile([P, U], F32, name="page%d" % t, tag="slot%d" % t, align_bytes=64) for t in range(PACK)]
+        for t in range(PACK):
+            nc.sync.dma_start(page[t][:], mem_rows[:, t, :])
+
+        sums = {}
 
         def add_turned(b, t, src, start, stop):
             nc.tensor.matmul(sums[b][:, t, :], lhsT=src, rhs=ident[:], is_transpose=True, start=start, stop=stop)
 
-        def plain_terms(hf):
+        def plain_terms(b, bank):
+            sums[b] = banks.tile([P, PACK, P], F32, name="sum%d" % b, tag=bank)
             for t in range(PACK):
-                for b in (2 * hf, 2 * hf + 1):
-                    add_turned(b, t, nd[t][:, b * P : (b + 1) * P], t == 0, False)
-                    add_turned(b, t, y[t][:, b * P : (b + 1) * P], False, False)
+                add_turned(b, t, nd[t][:, b * P : (b + 1) * P], t == 0, False)
+                add_turned(b, t, y[t][:, b * P : (b + 1) * P], False, False)
 
-        zi = [work.tile([P, HALF, PACK], BF16, name="zi%d" % hf, tag="zi%d" % hf, bufs=1, align_bytes=64) for hf in range(2)]
+        zi = [keep.tile([P, HALF, PACK], BF16, name="zi%d" % hf, tag="zi%d" % hf, align_bytes=64) for hf in range(2)]
 
-        def looked_up_terms(hf, t):
+        def looked_up_terms(hf, t, pre_tag, cut_tag):
             cols = slice(hf * HALF, (hf + 1) * HALF)
             lc = slice(hf * HALF // 16, (hf + 1) * HALF // 16)
-            if (hf, t) == (1, PACK - 1):
-                pre = work.tile([P, 2, HALF], F32, name="pre_last", tag="zi0", bufs=1, align_bytes=64)
-            else:
-                pre = work.tile([P, 2, HALF], F32, name="pre", bufs=4)
+            pre = keep.tile([P, 2, HALF], F32, name="pre", tag=pre_tag, align_bytes=64)
             nc.vector.tensor_tensor(pre[:, 0, :], y[t][:].indirect(n1_t[:, lc]), nd[t][:, cols], ALU.add)
             nc.vector.tensor_tensor(pre[:, 1, :], nd[t][:].indirect(n2_t[:, lc]), y[t][:, cols], ALU.add)
-            cut = work.tile([P, 2, HALF], F32, name="cut", bufs=4)
+            cut = keep.tile([P, 2, HALF], F32, name="cut", tag=cut_tag)
             nc.scalar.activation(cut[:], pre[:], ACT.Relu, scale=-1.0)
             for c in range(2):
                 for i in range(2):
@@ -142,7 +138,7 @@ def tile_picked_twlmaxbpage_none_po_kernel(tc, x_words, x_scales, w1_words, w1_s
         def quantise(hf):
             back = banks.tile([P, 2, HALF], F32, name="back")
             for c in range(2):
-                zt = work.tile([P, S], BF16, name="zt", bufs=2)
+                zt = keep.tile([P, S], BF16, name="zt", tag="zt%d" % (2 * hf + c))
                 nc.scalar.copy(zt[:].rearrange("j (u p e) -> j u p e", u=2, e=2), sums[2 * hf + c][:].rearrange("j (u e) p -> j u p e", u=2))
                 for u in range(2):
                     nc.tensor.transpose(back[:, u, c * P : (c + 1) * P], zt[:].bitcast(F32)[:, u * P : (u + 1) * P], ident[:])
@@ -154,41 +150,36 @@ def tile_picked_twlmaxbpage_none_po_kernel(tc, x_words, x_scales, w1_words, w1_s
             )
             nc.vector.quantize_mx(out=zq[hf][:].bitcast(FP8X4), scales=zs[hf][:], in_=zi[hf][:].rearrange("p j t -> p (j t)"))
 
-        h = [[None] * PACK, [None] * PACK]
+        h = [keep.tile([P, 2, S], F32, name="h%d" % u) for u in range(2)]
 
-        def second_product(hf, u):
-            if (hf, u) == (0, 1):
-                acc = banks.tile([P, 2, HALF], F32, name="acc_late", tag="sum3")
-            else:
-                acc = psum.tile([P, 2, HALF], F32, name="acc")
+        def second_product(hf, u, bank):
+            acc = banks.tile([P, 2, HALF], F32, name="acc2", tag=bank)
             for e in range(2):
                 product(2, 2 * u + e, acc[:, e, :], zq[hf][:], zs[hf][:])
-            hs = keep.tile([P, 2, HALF], F32, name="hs%d_%d" % (hf, u))
-            nc.scalar.copy(hs[:], acc[:])
-            h[hf][2 * u] = hs[:, 0, :]
-            h[hf][2 * u + 1] = hs[:, 1, :]
+            nc.scalar.copy(h[u][:, :, hf * HALF : (hf + 1) * HALF], acc[:])
 
-        plain_terms(0)
+        plain_terms(0, "d")
+        plain_terms(1, "e")
         for t in range(PACK):
-            looked_up_terms(0, t)
-        plain_terms(1)
+            looked_up_terms(0, t, "pre%d" % t, "cut%d" % t)
         quantise(0)
-        second_product(0, 0)
-        for t in range(PACK):
-            looked_up_terms(1, t)
+        second_product(0, 0, "a")
+        plain_terms(2, "c")
+        plain_terms(3, "d")
+        for t, pre_tag, cut_tag in ((0, "pre0", "zt0"), (1, "pre1", "zt1"), (2, "pre2", "zt0"), (3, "zi0", "cut3")):
+            looked_up_terms(1, t, pre_tag, cut_tag)
         quantise(1)
-        second_product(0, 1)
-        second_product(1, 0)
-        second_product(1, 1)
+        second_product(0, 1, "d")
+        second_product(1, 0, "b")
+        second_product(1, 1, "a")
 
         SPLIT = U // 2
         grouped = keep.tile([P, U, PACK], BF16, name="grouped", align_bytes=64)
         staged = keep.tile([P, PACK, SPLIT], BF16, name="staged", align_bytes=64)
         last = PACK - 1
-        for hf, t in ((0, 0), (0, 1), (0, 2), (1, 0), (1, 1), (1, 2), (0, 3), (1, 3)):
-            lc = slice(hf * HALF // 16, (hf + 1) * HALF // 16)
-            nc.vector.tensor_copy(page[t][:].indirect(n3_t[:, lc]), h[hf][t])
-            if hf == 1:
+        for t, lo, hi in ((0, 0, HALF), (1, 0, HALF), (2, 0, HALF), (0, HALF, S), (1, HALF, S), (2, HALF, S), (3, 0, S)):
+            nc.vector.tensor_copy(page[t][:].indirect(n3_t[:, lo // 16 : hi // 16]), h[t // 2][:, t % 2, lo:hi])
+            if hi == S:
                 nc.sync.dma_start(out_rows[:, t, :], page[t][:])
                 if t < last:
                     nc.scalar.copy(staged[:, t, :], page[t][:, :SPLIT])
@@ -202,9 +193,10 @@ def tile_picked_twlmaxbpage_none_po_kernel(tc, x_words, x_scales, w1_words, w1_s
             nc.scalar.copy(grouped[:, c * Q : (c + 1) * Q, last], page[last][:, c * Q : (c + 1) * Q])
         for c in (0, 1):
             nc.vector.tensor_copy(grouped[:, c * Q : (c + 1) * Q, :].rearrange("p (c i) t -> p c t i", i=4), staged[:, :, c * Q : (c + 1) * Q].rearrange("p t (c i) -> p c t i", i=4))
-        for c in (2, 0, 3, 1):
+        for c, lo, hi in ((2, 0, 0), (0, 0, Q), (3, 2 * Q, U), (1, Q, 2 * Q)):
             cs = slice(c * Q, (c + 1) * Q)
             nc.vector.quantize_mx(out=oq[:, cs].bitcast(FP8X4), scales=osc[:, cs], in_=grouped[:, cs, :].rearrange("p j t -> p (j t)"))
-            nc.sync.dma_start(words_out[:, cs], oq[:, cs].bitcast(I32))
+            if hi > lo:
+                nc.sync.dma_start(words_out[:, lo:hi], oq[:, lo:hi].bitcast(I32))
         for q in range(4):
             nc.scalar.dma_start(out_2[0, 4 * q : 4 * q + 4, :].bitcast(I32), osc[32 * q : 32 * q + 4, :].bitcast(I32))

@@ -18,22 +18,27 @@ P = 128
 PACK = 4
 T, S, U = 2048, 512, 1024
 HALF = S // 2
+PER_COLUMN = 16
+QUADRANTS = 4
 FLOPS = 3 * 2 * 512 * 512 * 512
 
 
-def tile_picked_twlmaxbpage_none_po_kernel(tc, x_words, x_scales, w1_words, w1_scales, w2_words, w2_scales, gn, w3_words, w3_scales, mem, offs, two, n1, n2, n3, out_0, out_1, out_2):
+def tile_picked_twlmaxbpage_none_po_kernel(
+    tc, x_words, x_scales, w1_words, w1_scales, w2_words, w2_scales, gn, w3_words, w3_scales, mem, offs, two, n1, n2, n3,
+    out_0, out_1, out_2,
+):
     nc = tc.nc
     with ExitStack() as ctx:
         keep = ctx.enter_context(tc.tile_pool(name="keep", bufs=1))
         banks = ctx.enter_context(tc.psum_pool(name="banks", bufs=1))
 
         def load_list(src, name):
-            t = keep.tile([P, S // 16], U16, name=name)
-            nc.sync.dma_start(t[:], src)
-            return t
+            tile = keep.tile([P, S // PER_COLUMN], U16, name=name)
+            nc.sync.dma_start(tile[:], src)
+            return tile
 
         def load_scale_rows(dst, src):
-            for q in range(4):
+            for q in range(QUADRANTS):
                 nc.sync.dma_start(dst[32 * q : 32 * q + 4, :].bitcast(I32), src[0, 4 * q : 4 * q + 4, :].bitcast(I32))
 
         xs = keep.tile([P, T], U8, name="xs", align_bytes=64)
@@ -43,7 +48,7 @@ def tile_picked_twlmaxbpage_none_po_kernel(tc, x_words, x_scales, w1_words, w1_s
             nc.vector.memset(ws_raw[i][:].bitcast(I32), 0)
 
         xw = keep.tile([P, T], I32, name="xw", tag="xw", align_bytes=64)
-        ww_raw = [keep.tile([P, 2 * S], U8, name="ww_raw%d" % i, tag=("slot2", "ww_raw1")[i], align_bytes=64) for i in range(2)]
+        ww_raw = [keep.tile([P, 2 * S], U8, name="ww_raw%d" % i, tag=("ww_raw0", "ww_raw1", "slot2")[i], align_bytes=64) for i in range(3)]
         offs_t = load_list(offs, "offs_t")
         two_t = load_list(two, "two_t")
         nc.sync.dma_start(ww_raw[0][:].bitcast(I32), w1_words[0].bitcast(I32))
@@ -54,37 +59,47 @@ def tile_picked_twlmaxbpage_none_po_kernel(tc, x_words, x_scales, w1_words, w1_s
         load_scale_rows(ws_raw[0], w1_scales)
         nc.sync.dma_start(ww_raw[1][:].bitcast(I32), w2_words[0].bitcast(I32))
         load_scale_rows(ws_raw[1], w2_scales)
+        nc.sync.dma_start(ww_raw[2][:].bitcast(I32), w3_words[0].bitcast(I32))
         n1_t = load_list(n1, "n1_t")
         n2_t = load_list(n2, "n2_t")
+        load_scale_rows(ws_raw[2], w3_scales)
+        n3_t = load_list(n3, "n3_t")
 
         ww, ws = [], []
 
         def deal(i, engine):
             ww.append(keep.tile([P, 2 * S], U8, name="ww%d" % i, tag=("ww0", "ww1", "xw")[i], align_bytes=64))
             ws.append(keep.tile([P, S], U8, name="ws%d" % i, tag=("ws0", "ws1", "sg0")[i], align_bytes=64))
-            engine.tensor_copy(ww[i][:].rearrange("p (t m b) -> p t m b", t=PACK, b=2), ww_raw[i][:].rearrange("p (m t b) -> p t m b", t=PACK, b=2))
+            engine.tensor_copy(
+                ww[i][:].rearrange("p (t m b) -> p t m b", t=PACK, b=2),
+                ww_raw[i][:].rearrange("p (m t b) -> p t m b", t=PACK, b=2),
+            )
             engine.tensor_copy(ws[i][:].rearrange("p (t m) -> p t m", t=PACK), ws_raw[i][:].rearrange("p (m t) -> p t m", t=PACK))
 
         deal(0, nc.gpsimd)
         deal(1, nc.gpsimd)
-        ww_raw.append(keep.tile([P, 2 * S], U8, name="ww_raw2", tag="slot2", align_bytes=64))
-        nc.sync.dma_start(ww_raw[2][:].bitcast(I32), w3_words[0].bitcast(I32))
-        load_scale_rows(ws_raw[2], w3_scales)
-        n3_t = load_list(n3, "n3_t")
 
-        lists = [offs_t, two_t]
+        picks = [offs_t, two_t]
         xg = [keep.tile([P, S], U32, name="xg%d" % i, tag="slot%d" % i, align_bytes=64) for i in range(2)]
         sg = [keep.tile([P, S], U8, name="sg%d" % i, tag="sg%d" % i, align_bytes=64) for i in range(2)]
         for i in range(2):
-            nc.vector.tensor_copy(sg[i][:], xs[:].indirect(lists[i][:]))
+            nc.vector.tensor_copy(sg[i][:], xs[:].indirect(picks[i][:]))
         for i in range(2):
-            nc.vector.tensor_copy(xg[i][:], xw[:].bitcast(U32).indirect(lists[i][:]))
+            nc.vector.tensor_copy(xg[i][:], xw[:].bitcast(U32).indirect(picks[i][:]))
 
         mem_rows = mem.rearrange("(p t) w -> p t w", t=PACK)
         out_rows = out_0.rearrange("(p t) w -> p t w", t=PACK)
 
         def product(i, t, acc, codes, scales):
-            nc.tensor.matmul_mx(out=acc, lhsT=ww[i][:, 2 * P * t : 2 * P * (t + 1)].bitcast(FP4X4), lhsT_scale=ws[i][:, P * t : P * (t + 1)], rhs=codes.bitcast(FP8X4), rhs_scale=scales, start=True, stop=True)
+            nc.tensor.matmul_mx(
+                out=acc,
+                lhsT=ww[i][:, 2 * P * t : 2 * P * (t + 1)].bitcast(FP4X4),
+                lhsT_scale=ws[i][:, P * t : P * (t + 1)],
+                rhs=codes.bitcast(FP8X4),
+                rhs_scale=scales,
+                start=True,
+                stop=True,
+            )
 
         ident = keep.tile([P, P], F32, name="ident")
         make_identity(nc, ident[:])
@@ -103,6 +118,7 @@ def tile_picked_twlmaxbpage_none_po_kernel(tc, x_words, x_scales, w1_words, w1_s
             nc.scalar.activation((y, nd)[i][t][:], acc[:], ACT.Copy, scale=(mag, neg)[i][:, t : t + 1])
 
         deal(2, nc.vector)
+
         page = [keep.tile([P, U], F32, name="page%d" % t, tag="slot%d" % t, align_bytes=64) for t in range(PACK)]
         for t in range(PACK):
             nc.sync.dma_start(page[t][:], mem_rows[:, t, :])
@@ -121,16 +137,16 @@ def tile_picked_twlmaxbpage_none_po_kernel(tc, x_words, x_scales, w1_words, w1_s
         zi = [keep.tile([P, HALF, PACK], BF16, name="zi%d" % hf, tag="zi%d" % hf, align_bytes=64) for hf in range(2)]
 
         def looked_up_terms(hf, t, pre_tag, cut_tag):
-            cols = slice(hf * HALF, (hf + 1) * HALF)
-            lc = slice(hf * HALF // 16, (hf + 1) * HALF // 16)
+            entries = slice(hf * HALF, (hf + 1) * HALF)
+            list_cols = slice(hf * HALF // PER_COLUMN, (hf + 1) * HALF // PER_COLUMN)
             pre = keep.tile([P, 2, HALF], F32, name="pre", tag=pre_tag, align_bytes=64)
-            nc.vector.tensor_tensor(pre[:, 0, :], y[t][:].indirect(n1_t[:, lc]), nd[t][:, cols], ALU.add)
-            nc.vector.tensor_tensor(pre[:, 1, :], nd[t][:].indirect(n2_t[:, lc]), y[t][:, cols], ALU.add)
+            nc.vector.tensor_tensor(pre[:, 0, :], y[t][:].indirect(n1_t[:, list_cols]), nd[t][:, entries], ALU.add)
+            nc.vector.tensor_tensor(pre[:, 1, :], nd[t][:].indirect(n2_t[:, list_cols]), y[t][:, entries], ALU.add)
             cut = keep.tile([P, 2, HALF], F32, name="cut", tag=cut_tag)
             nc.scalar.activation(cut[:], pre[:], ACT.Relu, scale=-1.0)
             for c in range(2):
-                for i in range(2):
-                    add_turned(2 * hf + c, t, cut[:, i, c * P : (c + 1) * P], False, t == PACK - 1 and i == 1)
+                for term in range(2):
+                    add_turned(2 * hf + c, t, cut[:, term, c * P : (c + 1) * P], False, t == PACK - 1 and term == 1)
 
         zq = [keep.tile([P, HALF], U32, name="zq%d" % hf, align_bytes=64) for hf in range(2)]
         zs = [keep.tile([P, HALF], U8, name="zs%d" % hf, align_bytes=64) for hf in range(2)]
@@ -139,7 +155,10 @@ def tile_picked_twlmaxbpage_none_po_kernel(tc, x_words, x_scales, w1_words, w1_s
             back = banks.tile([P, 2, HALF], F32, name="back")
             for c in range(2):
                 zt = keep.tile([P, S], BF16, name="zt", tag="zt%d" % (2 * hf + c))
-                nc.scalar.copy(zt[:].rearrange("j (u p e) -> j u p e", u=2, e=2), sums[2 * hf + c][:].rearrange("j (u e) p -> j u p e", u=2))
+                nc.scalar.copy(
+                    zt[:].rearrange("j (u p e) -> j u p e", u=2, e=2),
+                    sums[2 * hf + c][:].rearrange("j (u e) p -> j u p e", u=2),
+                )
                 for u in range(2):
                     nc.tensor.transpose(back[:, u, c * P : (c + 1) * P], zt[:].bitcast(F32)[:, u * P : (u + 1) * P], ident[:])
             nc.vector.tensor_tensor(
@@ -153,10 +172,10 @@ def tile_picked_twlmaxbpage_none_po_kernel(tc, x_words, x_scales, w1_words, w1_s
         h = [keep.tile([P, 2, S], F32, name="h%d" % u) for u in range(2)]
 
         def second_product(hf, u, bank):
-            acc = banks.tile([P, 2, HALF], F32, name="acc2", tag=bank)
+            acc2 = banks.tile([P, 2, HALF], F32, name="acc2", tag=bank)
             for e in range(2):
-                product(2, 2 * u + e, acc[:, e, :], zq[hf][:], zs[hf][:])
-            nc.scalar.copy(h[u][:, :, hf * HALF : (hf + 1) * HALF], acc[:])
+                product(2, 2 * u + e, acc2[:, e, :], zq[hf][:], zs[hf][:])
+            nc.scalar.copy(h[u][:, :, hf * HALF : (hf + 1) * HALF], acc2[:])
 
         plain_terms(0, "d")
         plain_terms(1, "e")
@@ -177,26 +196,45 @@ def tile_picked_twlmaxbpage_none_po_kernel(tc, x_words, x_scales, w1_words, w1_s
         grouped = keep.tile([P, U, PACK], BF16, name="grouped", align_bytes=64)
         staged = keep.tile([P, PACK, SPLIT], BF16, name="staged", align_bytes=64)
         last = PACK - 1
-        for t, lo, hi in ((0, 0, HALF), (1, 0, HALF), (2, 0, HALF), (0, HALF, S), (1, HALF, S), (2, HALF, S), (3, 0, S)):
-            nc.vector.tensor_copy(page[t][:].indirect(n3_t[:, lo // 16 : hi // 16]), h[t // 2][:, t % 2, lo:hi])
+        pieces = [(t, lo, lo + HALF) for lo in (0, HALF) for t in range(last)] + [(last, 0, S)]
+        for t, lo, hi in pieces:
+            nc.vector.tensor_copy(page[t][:].indirect(n3_t[:, lo // PER_COLUMN : hi // PER_COLUMN]), h[t // 2][:, t % 2, lo:hi])
             if hi == S:
                 nc.sync.dma_start(out_rows[:, t, :], page[t][:])
                 if t < last:
                     nc.scalar.copy(staged[:, t, :], page[t][:, :SPLIT])
                     nc.scalar.copy(grouped[:, SPLIT:, t], page[t][:, SPLIT:])
+
         oq = keep.tile([P, U], U32, name="oq", align_bytes=64)
         osc = keep.tile([P, U], U8, name="osc", align_bytes=64)
         words_out = out_1[0].rearrange("p n t -> p (n t)").bitcast(I32)
-        Q = U // 4
+        QUARTER = U // 4
+        quarter = [slice(c * QUARTER, (c + 1) * QUARTER) for c in range(4)]
         nc.vector.tensor_copy(staged[:, last, :], page[last][:, :SPLIT])
         for c in (2, 3):
-            nc.scalar.copy(grouped[:, c * Q : (c + 1) * Q, last], page[last][:, c * Q : (c + 1) * Q])
+            nc.scalar.copy(grouped[:, quarter[c], last], page[last][:, quarter[c]])
         for c in (0, 1):
-            nc.vector.tensor_copy(grouped[:, c * Q : (c + 1) * Q, :].rearrange("p (c i) t -> p c t i", i=4), staged[:, :, c * Q : (c + 1) * Q].rearrange("p t (c i) -> p c t i", i=4))
-        for c, lo, hi in ((2, 0, 0), (0, 0, Q), (3, 2 * Q, U), (1, Q, 2 * Q)):
-            cs = slice(c * Q, (c + 1) * Q)
-            nc.vector.quantize_mx(out=oq[:, cs].bitcast(FP8X4), scales=osc[:, cs], in_=grouped[:, cs, :].rearrange("p j t -> p (j t)"))
-            if hi > lo:
-                nc.sync.dma_start(words_out[:, lo:hi], oq[:, lo:hi].bitcast(I32))
-        for q in range(4):
+            nc.vector.tensor_copy(
+                grouped[:, quarter[c], :].rearrange("p (c i) t -> p c t i", i=4),
+                staged[:, :, quarter[c]].rearrange("p t (c i) -> p c t i", i=4),
+            )
+
+        def quantise_out(c):
+            nc.vector.quantize_mx(
+                out=oq[:, quarter[c]].bitcast(FP8X4),
+                scales=osc[:, quarter[c]],
+                in_=grouped[:, quarter[c], :].rearrange("p j t -> p (j t)"),
+            )
+
+        def store_words(cols):
+            nc.sync.dma_start(words_out[:, cols], oq[:, cols].bitcast(I32))
+
+        quantise_out(2)
+        quantise_out(0)
+        store_words(quarter[0])
+        quantise_out(3)
+        store_words(slice(SPLIT, U))
+        quantise_out(1)
+        store_words(quarter[1])
+        for q in range(QUADRANTS):
             nc.scalar.dma_start(out_2[0, 4 * q : 4 * q + 4, :].bitcast(I32), osc[32 * q : 32 * q + 4, :].bitcast(I32))

from contextlib import ExitStack

import concourse.mybir as mybir
from concourse.masks import make_identity

F32 = mybir.dt.float32
BF16 = mybir.dt.bfloat16
I32 = mybir.dt.int32
U32 = mybir.dt.uint32
U16 = mybir.dt.uint16
U8 = mybir.dt.uint8
FP8X4 = mybir.dt.float8_e4m3fn_x4
FP4X4 = mybir.dt.float4_e2m1fn_x4
ALU = mybir.AluOpType
ACT = mybir.ActivationFunctionType

P = 128
PACK = 4
T, S, U = 2048, 512, 1024
HALF = S // 2
PER_COLUMN = 16
QUADRANTS = 4
FLOPS = 3 * 2 * 512 * 512 * 512


def tile_picked_twlmaxbpage_none_po_kernel(
    tc, x_words, x_scales, w1_words, w1_scales, w2_words, w2_scales, gn, w3_words, w3_scales, mem, offs, two, n1, n2, n3,
    out_0, out_1, out_2,
):
    nc = tc.nc
    with ExitStack() as ctx:
        keep = ctx.enter_context(tc.tile_pool(name="keep", bufs=1))
        banks = ctx.enter_context(tc.psum_pool(name="banks", bufs=1))

        def load_list(src, name):
            tile = keep.tile([P, S // PER_COLUMN], U16, name=name)
            nc.sync.dma_start(tile[:], src)
            return tile

        def load_scale_rows(dst, src):
            for q in range(QUADRANTS):
                nc.sync.dma_start(dst[32 * q : 32 * q + 4, :].bitcast(I32), src[0, 4 * q : 4 * q + 4, :].bitcast(I32))

        xs = keep.tile([P, T], U8, name="xs", align_bytes=64)
        nc.vector.memset(xs[:].bitcast(I32), 0)
        ws_raw = [keep.tile([P, S], U8, name="ws_raw%d" % i, tag=("ws_raw0", "ws_raw1", "slot3")[i], align_bytes=64) for i in range(3)]
        for i in range(3):
            nc.vector.memset(ws_raw[i][:].bitcast(I32), 0)

        xw = keep.tile([P, T], I32, name="xw", tag="xw", align_bytes=64)
        ww_raw = [keep.tile([P, 2 * S], U8, name="ww_raw%d" % i, tag=("ww_raw0", "ww_raw1", "slot2")[i], align_bytes=64) for i in range(3)]
        offs_t = load_list(offs, "offs_t")
        two_t = load_list(two, "two_t")
        nc.sync.dma_start(ww_raw[0][:].bitcast(I32), w1_words[0].bitcast(I32))
        load_scale_rows(xs, x_scales)
        nc.sync.dma_start(xw[:], x_words[0].rearrange("p n t -> p (n t)").bitcast(I32))
        gn_t = keep.tile([P, PACK], F32, name="gn_t")
        nc.gpsimd.dma_start(gn_t[:], gn.rearrange("(p t) o -> p (t o)", t=PACK))
        load_scale_rows(ws_raw[0], w1_scales)
        nc.sync.dma_start(ww_raw[1][:].bitcast(I32), w2_words[0].bitcast(I32))
        load_scale_rows(ws_raw[1], w2_scales)
        nc.sync.dma_start(ww_raw[2][:].bitcast(I32), w3_words[0].bitcast(I32))
        n1_t = load_list(n1, "n1_t")
        n2_t = load_list(n2, "n2_t")
        load_scale_rows(ws_raw[2], w3_scales)
        n3_t = load_list(n3, "n3_t")

        ww, ws = [], []

        def deal(i, engine):
            ww.append(keep.tile([P, 2 * S], U8, name="ww%d" % i, tag=("ww0", "ww1", "xw")[i], align_bytes=64))
            ws.append(keep.tile([P, S], U8, name="ws%d" % i, tag=("ws0", "ws1", "sg0")[i], align_bytes=64))
            engine.tensor_copy(
                ww[i][:].rearrange("p (t m b) -> p t m b", t=PACK, b=2),
                ww_raw[i][:].rearrange("p (m t b) -> p t m b", t=PACK, b=2),
            )
            engine.tensor_copy(ws[i][:].rearrange("p (t m) -> p t m", t=PACK), ws_raw[i][:].rearrange("p (m t) -> p t m", t=PACK))

        deal(0, nc.gpsimd)
        deal(1, nc.gpsimd)

        picks = [offs_t, two_t]
        xg = [keep.tile([P, S], U32, name="xg%d" % i, tag="slot%d" % i, align_bytes=64) for i in range(2)]
        sg = [keep.tile([P, S], U8, name="sg%d" % i, tag="sg%d" % i, align_bytes=64) for i in range(2)]
        for i in range(2):
            nc.vector.tensor_copy(sg[i][:], xs[:].indirect(picks[i][:]))
        for i in range(2):
            nc.vector.tensor_copy(xg[i][:], xw[:].bitcast(U32).indirect(picks[i][:]))

        mem_rows = mem.rearrange("(p t) w -> p t w", t=PACK)
        out_rows = out_0.rearrange("(p t) w -> p t w", t=PACK)

        def product(i, t, acc, codes, scales):
            nc.tensor.matmul_mx(
                out=acc,
                lhsT=ww[i][:, 2 * P * t : 2 * P * (t + 1)].bitcast(FP4X4),
                lhsT_scale=ws[i][:, P * t : P * (t + 1)],
                rhs=codes.bitcast(FP8X4),
                rhs_scale=scales,
                start=True,
                stop=True,
            )

        ident = keep.tile([P, P], F32, name="ident")
        make_identity(nc, ident[:])
        mag = keep.tile([P, PACK], F32, name="mag")
        neg = keep.tile([P, PACK], F32, name="neg")
        sgn = keep.tile([P, PACK], BF16, name="sgn")
        nc.scalar.activation(mag[:], gn_t[:], ACT.Abs)
        nc.scalar.activation(neg[:], mag[:], ACT.Copy, scale=-1.0)
        nc.scalar.activation(sgn[:], gn_t[:], ACT.Sign)

        y = [keep.tile([P, S], F32, name="y%d" % t) for t in range(PACK)]
        nd = [keep.tile([P, S], F32, name="nd%d" % t) for t in range(PACK)]
        for i, t, bank in ((0, 0, "a"), (0, 1, "b"), (1, 0, "c"), (1, 1, "a"), (0, 2, "c"), (1, 2, "b"), (0, 3, "a"), (1, 3, "c")):
            acc = banks.tile([P, S], F32, name="acc", tag=bank)
            product(i, t, acc[:], xg[i][:], sg[i][:])
            nc.scalar.activation((y, nd)[i][t][:], acc[:], ACT.Copy, scale=(mag, neg)[i][:, t : t + 1])

        deal(2, nc.vector)

        page = [keep.tile([P, U], F32, name="page%d" % t, tag="slot%d" % t, align_bytes=64) for t in range(PACK)]
        for t in range(PACK):
            nc.sync.dma_start(page[t][:], mem_rows[:, t, :])

        sums = {}

        def add_turned(b, t, src, start, stop):
            nc.tensor.matmul(sums[b][:, t, :], lhsT=src, rhs=ident[:], is_transpose=True, start=start, stop=stop)

        def plain_terms(b, bank):
            sums[b] = banks.tile([P, PACK, P], F32, name="sum%d" % b, tag=bank)
            for t in range(PACK):
                add_turned(b, t, nd[t][:, b * P : (b + 1) * P], t == 0, False)
                add_turned(b, t, y[t][:, b * P : (b + 1) * P], False, False)

        zi = [keep.tile([P, HALF, PACK], BF16, name="zi%d" % hf, tag="zi%d" % hf, align_bytes=64) for hf in range(2)]

        def looked_up_terms(hf, t, pre_tag, cut_tag):
            entries = slice(hf * HALF, (hf + 1) * HALF)
            list_cols = slice(hf * HALF // PER_COLUMN, (hf + 1) * HALF // PER_COLUMN)
            pre = keep.tile([P, 2, HALF], F32, name="pre", tag=pre_tag, align_bytes=64)
            nc.vector.tensor_tensor(pre[:, 0, :], y[t][:].indirect(n1_t[:, list_cols]), nd[t][:, entries], ALU.add)
            nc.vector.tensor_tensor(pre[:, 1, :], nd[t][:].indirect(n2_t[:, list_cols]), y[t][:, entries], ALU.add)
            cut = keep.tile([P, 2, HALF], F32, name="cut", tag=cut_tag)
            nc.scalar.activation(cut[:], pre[:], ACT.Relu, scale=-1.0)
            for c in range(2):
                for term in range(2):
                    add_turned(2 * hf + c, t, cut[:, term, c * P : (c + 1) * P], False, t == PACK - 1 and term == 1)

        zq = [keep.tile([P, HALF], U32, name="zq%d" % hf, align_bytes=64) for hf in range(2)]
        zs = [keep.tile([P, HALF], U8, name="zs%d" % hf, align_bytes=64) for hf in range(2)]

        def quantise(hf):
            back = banks.tile([P, 2, HALF], F32, name="back")
            for c in range(2):
                zt = keep.tile([P, S], BF16, name="zt", tag="zt%d" % (2 * hf + c))
                nc.scalar.copy(
                    zt[:].rearrange("j (u p e) -> j u p e", u=2, e=2),
                    sums[2 * hf + c][:].rearrange("j (u e) p -> j u p e", u=2),
                )
                for u in range(2):
                    nc.tensor.transpose(back[:, u, c * P : (c + 1) * P], zt[:].bitcast(F32)[:, u * P : (u + 1) * P], ident[:])
            nc.vector.tensor_tensor(
                zi[hf][:].rearrange("p j (u e) -> p j u e", u=2),
                back[:].rearrange("p u j -> p (u j)").bitcast(BF16).rearrange("p (u j e) -> p j u e", u=2, e=2),
                sgn[:].rearrange("p (u e) -> p u e", u=2).unsqueeze(1).to_broadcast([P, HALF, 2, 2]),
                ALU.mult,
            )
            nc.vector.quantize_mx(out=zq[hf][:].bitcast(FP8X4), scales=zs[hf][:], in_=zi[hf][:].rearrange("p j t -> p (j t)"))

        h = [keep.tile([P, 2, S], F32, name="h%d" % u) for u in range(2)]

        def second_product(hf, u, bank):
            acc2 = banks.tile([P, 2, HALF], F32, name="acc2", tag=bank)
            for e in range(2):
                product(2, 2 * u + e, acc2[:, e, :], zq[hf][:], zs[hf][:])
            nc.scalar.copy(h[u][:, :, hf * HALF : (hf + 1) * HALF], acc2[:])

        plain_terms(0, "d")
        plain_terms(1, "e")
        for t in range(PACK):
            looked_up_terms(0, t, "pre%d" % t, "cut%d" % t)
        quantise(0)
        second_product(0, 0, "a")
        plain_terms(2, "c")
        plain_terms(3, "d")
        for t, pre_tag, cut_tag in ((0, "pre0", "zt0"), (1, "pre1", "zt1"), (2, "pre2", "zt0"), (3, "zi0", "cut3")):
            looked_up_terms(1, t, pre_tag, cut_tag)
        quantise(1)
        second_product(0, 1, "d")
        second_product(1, 0, "b")
        second_product(1, 1, "a")

        SPLIT = U // 2
        grouped = keep.tile([P, U, PACK], BF16, name="grouped", align_bytes=64)
        staged = keep.tile([P, PACK, SPLIT], BF16, name="staged", align_bytes=64)
        last = PACK - 1
        pieces = [(t, lo, lo + HALF) for lo in (0, HALF) for t in range(last)] + [(last, 0, S)]
        for t, lo, hi in pieces:
            nc.vector.tensor_copy(page[t][:].indirect(n3_t[:, lo // PER_COLUMN : hi // PER_COLUMN]), h[t // 2][:, t % 2, lo:hi])
            if hi == S:
                nc.sync.dma_start(out_rows[:, t, :], page[t][:])
                if t < last:
                    nc.scalar.copy(staged[:, t, :], page[t][:, :SPLIT])
                    nc.scalar.copy(grouped[:, SPLIT:, t], page[t][:, SPLIT:])

        oq = keep.tile([P, U], U32, name="oq", align_bytes=64)
        osc = keep.tile([P, U], U8, name="osc", align_bytes=64)
        words_out = out_1[0].rearrange("p n t -> p (n t)").bitcast(I32)
        QUARTER = U // 4
        quarter = [slice(c * QUARTER, (c + 1) * QUARTER) for c in range(4)]
        nc.vector.tensor_copy(staged[:, last, :], page[last][:, :SPLIT])
        for c in (2, 3):
            nc.scalar.copy(grouped[:, quarter[c], last], page[last][:, quarter[c]])
        for c in (0, 1):
            nc.vector.tensor_copy(
                grouped[:, quarter[c], :].rearrange("p (c i) t -> p c t i", i=4),
                staged[:, :, quarter[c]].rearrange("p t (c i) -> p c t i", i=4),
            )

        def quantise_out(c):
            nc.vector.quantize_mx(
                out=oq[:, quarter[c]].bitcast(FP8X4),
                scales=osc[:, quarter[c]],
                in_=grouped[:, quarter[c], :].rearrange("p j t -> p (j t)"),
            )

        def store_words(cols):
            nc.sync.dma_start(words_out[:, cols], oq[:, cols].bitcast(I32))

        quantise_out(2)
        quantise_out(0)
        store_words(quarter[0])
        quantise_out(3)
        store_words(slice(SPLIT, U))
        quantise_out(1)
        store_words(quarter[1])
        for q in range(QUADRANTS):
            nc.scalar.dma_start(out_2[0, 4 * q : 4 * q + 4, :].bitcast(I32), osc[32 * q : 32 * q + 4, :].bitcast(I32))
